import numpy as np, ml_dtypes
CORES = [3,11,19,27,35,43]
N = 6
import mx_ref
BF = ml_dtypes.bfloat16
def entries(a):
    return np.ascontiguousarray(a.T).reshape(-1)
def table(e):
    return np.ascontiguousarray(np.reshape(e, (-1, 16)).T).astype(np.int32)
def cols(t, e):
    v = np.concatenate([t.reshape(128, -1, 4), np.zeros((128, 1, 4), BF)], axis=1)
    return np.ascontiguousarray(v[:, e]).reshape(128, -1)
def tile(rs):
    return np.stack(rs, axis=2).reshape(128, -1).astype(BF)
def cut(t, i, w=512):
    return t[:, w * i:w * i + w]
def f(rng, *shape):
    return mx_ref.flush((rng.standard_normal(shape, dtype=np.float32) * np.exp2(rng.integers(-2, 3, shape[:-1] + (1,)))).astype(BF))
def wide(rng, *shape, cols=0):
    v = rng.standard_normal(shape, dtype=np.float32) * np.exp2(rng.integers(-12, 13, shape)).astype(np.float32)
    if cols: v *= np.repeat(np.exp2(rng.integers(-cols, cols + 1, shape[:-2] + (1, shape[-1] // 4))) * (rng.random(shape[:-2] + (1, shape[-1] // 4)) > 0.0625), 4, axis=-1).astype(np.float32)
    return mx_ref.flush(v.astype(BF))
T, P, CAPP = 128, 192, 32
BASE = T + 3 * P
def sends(a):
    return entries(a).reshape(3, N, CAPP)
def filled(s, r, t):
    return s[:, :t, r].transpose(1, 0, 2).reshape(-1) >= 0
def lists(rng, how=""):
    s = np.full((N, 3, N, CAPP), -1)
    a = int(rng.integers(0, N)); same = (a, int(rng.integers(0, 3)), (a + int(rng.integers(1, N))) % N)
    for t in range(3):
        for q in range(N):
            got = BASE + np.flatnonzero(filled(s, q, t))
            for r in range(N):
                if q == r: continue
                least = 1 if t == 0 and r == (q + 1) % N else 0
                k = rng.permutation(CAPP)[:CAPP if how == "far" else rng.integers(least, CAPP + 1)]
                e = rng.integers(T + (t - 1) * P if how == "far" and t > 0 else 0, T + t * P, len(k))
                if t > 0:
                    m = (len(k) + 1) // 2; e[:m] = got[rng.integers(0, len(got), m)]
                s[q, t, r, k] = e
                if how == "shared" and (q, t, r) == same: s[q, t, r] = rng.integers(0, T + t * P)
    c = np.zeros((N, 2, 3, P), int)
    for r in range(N):
        for t in range(3):
            low = 2 if how == "skip" and t == 2 else t + 1
            own = T + (low - 1) * P; got = BASE + np.flatnonzero(filled(s, r, low))
            for h in range(2):
                c[r, h, t] = rng.integers(0, own, P)
                if len(got):
                    there = np.ones(P, bool) if how == "far" else rng.random(P) < 0.5
                    c[r, h, t] = np.where(there, got[rng.integers(0, len(got), P)], c[r, h, t])
            if how == "shared":
                one = int(c[r, 0, t, 0]); k = rng.permutation(P)
                c[r, 0, t, k[:P - P // 8]] = one; c[r, 1, t, k[:P // 8]] = one
            if how == "chains":
                c[r, 0, t] = np.arange(P) % T if t == 0 else T + (t - 1) * P + np.arange(P)
                c[r, 1, t] = rng.integers(0, T, P)
    return {"sn": np.stack([table(s[r]) for r in range(N)]), "lc": np.stack([table(c[r, 0]) for r in range(N)]), "rc": np.stack([table(c[r, 1]) for r in range(N)])}
def setup_inputs(rng):
    return {"x": f(rng, N, 128, 4 * T), "wl": np.stack([f(rng, 128, 2048)] * N), "wr": np.stack([f(rng, 128, 2048)] * N), "v": f(rng, N, 128, 512), **lists(rng)}
def setup_inputs_chains(rng):
    return {**setup_inputs(rng), **lists(rng, "chains")}
def setup_inputs_far(rng):
    return {**setup_inputs(rng), **lists(rng, "far")}
def setup_inputs_shared(rng):
    return {**setup_inputs(rng), **lists(rng, "shared")}
def setup_inputs_skip(rng):
    return {**setup_inputs(rng), **lists(rng, "skip")}
def setup_inputs_spread(rng):
    d = setup_inputs(rng); d["x"] = wide(rng, N, 128, 4 * T, cols=8); return d
def check_inputs(d):
    b = []
    for n in ("wl", "wr"):
        if any((d[n][r] != d[n][0]).any() for r in range(N)): b.append(n)
    s = np.stack([sends(d["sn"][r]) for r in range(N)])
    for r in range(N):
        for t in range(3):
            own = np.concatenate([np.ones(T + t * P, bool), np.zeros((3 - t) * P, bool)])
            ok = np.concatenate([own, filled(s, r, t)]); e = s[r, t]
            if e.min() < -1 or e.max() >= len(ok) or not ok[e[e >= 0]].all() or (s[r, t, r] != -1).any(): b.append("sn")
            ok = np.concatenate([own, filled(s, r, t + 1)])
            for n in ("lc", "rc"):
                e = entries(d[n][r])[t * P:t * P + P]
                if e.min() < 0 or e.max() >= len(ok) or not ok[e].all(): b.append(n)
    return b
def reference(x, wl, wr, v, sn, lc, rc):
    WL = [[mx_ref.quantize(np.ascontiguousarray(cut(wl[r], i))) for i in range(4)] for r in range(N)]
    WR = [[mx_ref.quantize(np.ascontiguousarray(cut(wr[r], i))) for i in range(4)] for r in range(N)]
    pool = [x[r] for r in range(N)]; slots = [[] for r in range(N)]
    for t in range(3):
        before = [np.concatenate([pool[r], np.zeros((128, 4 * (3 - t) * P), BF)] + slots[r], axis=1) for r in range(N)]
        for r in range(N):
            for q in range(N): slots[r].append(cols(before[q], sends(sn[q])[t, r]))
        made = []
        for r in range(N):
            known = np.concatenate([before[r]] + slots[r][t * N:], axis=1)
            left = mx_ref.quantize(cols(known, entries(lc[r])[t * P:t * P + P]))
            right = mx_ref.quantize(cols(known, entries(rc[r])[t * P:t * P + P]))
            made.append(tile([np.maximum(mx_ref.matmul(WL[r][i], left) + mx_ref.matmul(WR[r][i], right), np.float32(0)) * np.float32(0.05) for i in range(4)]))
        pool = [np.concatenate([pool[r], made[r]], axis=1) for r in range(N)]
    y = np.zeros((N, 128, P), np.float32)
    for r in range(N):
        y[r] = mx_ref.matmul(mx_ref.quantize(v[r]), mx_ref.quantize(np.ascontiguousarray(pool[r][:, 4 * (T + 2 * P):])))
    return {"y": y}

@@ -1,0 +1,287 @@
+from concourse.bass import DstId, RemoteDMATransfer
+from concourse.mybir import dt, AluOpType, ActivationFunctionType
+
+N, LEAVES, NODES, CAPP, LEVELS = 6, 128, 192, 32, 3
+BASE = LEAVES + LEVELS * NODES
+SENT = (N - 1) * CAPP
+F8 = "float8_e4m3fn_x4"
+KIDS = NODES // 16
+OFFS = SENT // 16
+KEPT = 2 * N * CAPP // 16
+
+SCRATCH = {
+    "xt": ("sbuf", [128, 4 * LEAVES], "bfloat16"),
+    "wlt": ("sbuf", [128, 2048], "bfloat16"),
+    "wrt": ("sbuf", [128, 2048], "bfloat16"),
+    "vt": ("sbuf", [128, 512], "bfloat16"),
+    "sni": ("sbuf", [128, LEVELS * N * 2], "int32"),
+    "lci": ("sbuf", [128, LEVELS * KIDS], "int32"),
+    "rci": ("sbuf", [128, LEVELS * KIDS], "int32"),
+    "pi": ("sbuf", [128, KEPT], "int32"),
+    "pm": ("sbuf", [128, KEPT], "int32"),
+    "ci": ("sbuf", [128, KEPT], "int32"),
+    "ki": ("sbuf", [128, KEPT], "int32"),
+    "ko": ("sbuf", [128, KEPT], "uint16"),
+    "so": ("sbuf", [128, LEVELS * OFFS], "uint16"),
+    "lo": ("sbuf", [128, LEVELS * KIDS], "uint16"),
+    "ro": ("sbuf", [128, LEVELS * KIDS], "uint16"),
+    "wlq": ("sbuf", [128, 512], F8), "wls": ("sbuf", [128, 512], "uint8"),
+    "wrq": ("sbuf", [128, 512], F8), "wrs": ("sbuf", [128, 512], "uint8"),
+    "vq": ("sbuf", [128, 128], F8), "vs": ("sbuf", [128, 128], "uint8"),
+    "hq": ("sbuf", [128, NODES], F8), "hs": ("sbuf", [128, NODES], "uint8"),
+    "ys": ("sbuf", [128, NODES], "float32"),
+    "psa": ("psum", [128, 2048], "float32"),
+    "psb": ("psum", [128, 2048], "float32"),
+}
+WIDE = {1: LEAVES, 2: BASE + N * CAPP, 3: BASE + 2 * N * CAPP, 4: BASE + 3 * N * CAPP}
+for _t in WIDE:
+    SCRATCH["w%dq" % _t] = ("sbuf", [128, WIDE[_t]], F8)
+    SCRATCH["w%ds" % _t] = ("sbuf", [128, WIDE[_t]], "uint8")
+for _t in (1, 2, 3):
+    SCRATCH["o%dq" % _t] = ("sbuf", [128, SENT], F8)
+    SCRATCH["o%ds" % _t] = ("sbuf", [128, SENT], "uint8")
+    SCRATCH["h%d" % _t] = ("sbuf", [128, 4 * NODES], "bfloat16")
+    for _n in ("l", "r"):
+        SCRATCH["%s%dq" % (_n, _t)] = ("sbuf", [128, NODES], F8)
+        SCRATCH["%s%ds" % (_n, _t)] = ("sbuf", [128, NODES], "uint8")
+
+SEMAPHORES = ["ldx", "ldsn", "ldwl", "ldwr", "ldv", "ldlc", "ldrc", "so1", "so1b", "so23", "clo", "cro",
+              "iot", "iom", "ioa", "cko",
+              "qx1", "qx2", "qx34", "qwl", "qwr", "qv", "own3", "own4", "kq3", "ks3", "kq4", "ks4", "left",
+              "qh", "mmy", "evy", "sty"]
+for _t in (1, 2, 3):
+    SEMAPHORES += ["%s%d" % (_n, _t) for _n in ("paq", "pas", "pbq", "pbs", "arq", "ars", "plq", "pls", "prq", "prs",
+                                                "evv", "evs", "qn")]
+    SEMAPHORES += ["mm%d_%d" % (_t, _i) for _i in range(4)]
+
+
+def order(topo, cores, s):
+    me = topo.chip(cores[s])
+    far, near, mate = [], [], []
+    for k in range(1, N):
+        d = (s + k) % N
+        c = topo.chip(cores[d])
+        (mate if topo.mates(me, c) else near if topo.same_plane(me, c) else far).append(d)
+    return far, near + mate
+
+
+def plan(topo, cores, s):
+    far, one = order(topo, cores, s)
+    e = topo.engines(cores[s], cores[far[0]])[:8]
+    a = [(d, k, e[4 * k:4 * k + 4]) for k, d in enumerate(far)]
+
+    def others(big, small):
+        return [(d, len(far) + k, es) for k, (d, es) in enumerate(zip(one, (big, small[:2], small[2:])))]
+    return [("q", "pa", a), ("s", "pa", a),
+            ("q", "pb", others(e[0::2], e[1::2])), ("s", "pb", others(e[1::2], e[0::2]))]
+
+
+def bits(es):
+    m = 0
+    for e in es:
+        m |= 1 << e
+    return m
+
+
+def rank_program(g, core, T, topo):
+    rank = T.rank_of(core)
+    if rank is None:
+        return
+    cores = list(T.cores)
+    S = T.sem
+    V, A, E, Y = g.vector, g.scalar, g.tensor, g.sync
+    RELU, COPY = ActivationFunctionType.Relu, ActivationFunctionType.Copy
+
+    def arrivals(form):
+        return sum(len(es) for s in range(N) if s != rank for f, _p, trs in plan(topo, cores, s) if f == form
+                   for d, _k, es in trs if d == rank)
+    NQ, NS = arrivals("q"), arrivals("s")
+
+    def runs_of(levels):
+        cuts = [-1] + [N * t + rank for t in range(levels)] + [N * levels]
+        return [(a + 1, b) for a, b in zip(cuts, cuts[1:]) if b > a + 1]
+    runs, runs2 = runs_of(1), runs_of(2)
+    far, one = order(topo, cores, rank)
+    CUT = len(far)
+
+    def table(q, out, src, groups, sem):
+        for k in groups:
+            q.dma_start(out[16 * k:16 * k + 16, :], src[:, :]).then_inc(sem, 16)
+    Y.dma_start(T.xt[:], T.x[:]).then_inc(S.ldx, 16)
+    table(A, T.sni, T.sn, range(0, 5), S.ldsn)
+    table(Y, T.sni, T.sn, range(5, 8), S.ldsn)
+    Y.dma_start(T.wlt[:], T.wl[:]).then_inc(S.ldwl, 16)
+    A.dma_start(T.wrt[:], T.wr[:]).then_inc(S.ldwr, 16)
+    table(Y, T.lci, T.lc, range(8), S.ldlc)
+    table(A, T.rci, T.rc, range(8), S.ldrc)
+    Y.dma_start(T.vt[:], T.v[:]).then_inc(S.ldv, 16)
+
+    def slots_list(t, ds, k, sem):
+        for d in ds:
+            at, of = OFFS * (t - 1) + 2 * k, 2 * (N * (t - 1) + d)
+            V.tensor_copy(T.so[:, at:at + 2], T.sni[:, of:of + 2]).then_inc(sem, 1)
+            k += 1
+
+    def quant(t, tile, at, n, sem):
+        V.quantize_mx(T["w%dq" % t][:, at:at + n], T["w%ds" % t][:, at:at + n], tile[:]).then_inc(sem, 1)
+
+    def pick_codes(name, at, n, t, off, a, b, sem):
+        V.tensor_copy(T[name + "q"][:, at:at + n].bitcast(dt.uint32),
+                      T["w%dq" % t][:, 0:WIDE[t]].bitcast(dt.uint32).indirect(off[:, a:b])).then_inc(sem, 1)
+
+    def pick_scales(name, at, n, t, off, a, b, sem):
+        A.activation(T[name + "s"][:, at:at + n], T["w%ds" % t][:, 0:WIDE[t]].indirect(off[:, a:b]), COPY).then_inc(sem, 1)
+
+    def pick_far(pick, t, sem):
+        pick("o%d" % t, 0, CUT * CAPP, t, T.so, OFFS * (t - 1), OFFS * (t - 1) + 2 * CUT, sem)
+
+    def pick_one(pick, t, sem):
+        pick("o%d" % t, CUT * CAPP, SENT - CUT * CAPP, t, T.so, OFFS * (t - 1) + 2 * CUT, OFFS * t, sem)
+
+    def keep(pick, rs, t, sem):
+        for a, b in rs:
+            pick("w%d" % (t + 1), BASE + a * CAPP, (b - a) * CAPP, t, T.ko, 2 * a, 2 * b, sem)
+
+    def bank(t, i):
+        return (T.psa if t % 2 else T.psb)[:, 512 * i:512 * i + NODES]
+
+    V.wait_ge(S.iot, 2)
+    V.tensor_scalar(T.pm[:], T.pi[:], 15, None, AluOpType.bitwise_and).then_inc(S.iom, 1)
+    V.wait_ge(S.iom, 1)
+    V.tensor_tensor(T.ki[:], T.pm[:], T.ci[:], AluOpType.add).then_inc(S.ioa, 1)
+    V.wait_ge(S.ioa, 1)
+    V.tensor_copy(T.ko[:], T.ki[:]).then_inc(S.cko, 1)
+
+    V.wait_ge(S.ldsn, 128)
+    slots_list(1, far, 0, S.so1)
+    V.wait_ge(S.ldx, 16)
+    quant(1, T.xt, 0, LEAVES, S.qx1)
+    V.wait_ge(S.so1, CUT)
+    V.wait_ge(S.qx1, 1)
+    pick_far(pick_codes, 1, S.paq1)
+    slots_list(1, one, CUT, S.so1b)
+    V.wait_ge(S.so1b, len(one))
+    pick_one(pick_codes, 1, S.pbq1)
+    quant(2, T.xt, 0, LEAVES, S.qx2)
+    quant(3, T.xt, 0, LEAVES, S.qx34)
+    quant(4, T.xt, 0, LEAVES, S.qx34)
+    for t in (2, 3):
+        slots_list(t, far + one, 0, S.so23)
+    V.wait_ge(S.ldwl, 16)
+    V.quantize_mx(T.wlq[:], T.wls[:], T.wlt[:]).then_inc(S.qwl, 1)
+    V.wait_ge(S.ldwr, 16)
+    V.quantize_mx(T.wrq[:], T.wrs[:], T.wrt[:]).then_inc(S.qwr, 1)
+    V.wait_ge(S.ldlc, 128)
+    V.tensor_copy(T.lo[:], T.lci[:]).then_inc(S.clo, 1)
+    V.wait_ge(S.ldrc, 128)
+    V.tensor_copy(T.ro[:], T.rci[:]).then_inc(S.cro, 1)
+
+    def ready(q, t):
+        if t == 1:
+            q.wait_ge(S.qx2, 1)
+            q.wait_ge(S.qx34, 2)
+            q.wait_ge(S.so23, 2 * (N - 1))
+            q.wait_ge(S.clo, 1)
+            q.wait_ge(S.cro, 1)
+            q.wait_ge(S.cko, 1)
+        if t == 2:
+            q.wait_ge(S.own3, 1)
+            q.wait_ge(S.kq3 if q is V else S.ks3, len(runs))
+        if t == 3:
+            q.wait_ge(S.own4, 2)
+            q.wait_ge(S.kq4 if q is V else S.ks4, len(runs2))
+
+    for t in (1, 2, 3):
+        ready(V, t)
+        V.wait_ge(S["arq%d" % t], NQ)
+        pick_codes("l%d" % t, 0, NODES, t + 1, T.lo, KIDS * (t - 1), KIDS * t, S["plq%d" % t])
+        pick_codes("r%d" % t, 0, NODES, t + 1, T.ro, KIDS * (t - 1), KIDS * t, S["prq%d" % t])
+        h = T["h%d" % t]
+        for i in (1, 3):
+            V.wait_ge(S["mm%d_%d" % (t, i)], 1)
+            V.tensor_scalar(h[:, i:4 * NODES:4], bank(t, i), 0.0, 0.05, AluOpType.max, AluOpType.mult).then_inc(S["evv%d" % t], 1)
+        V.wait_ge(S["evs%d" % t], 2)
+        V.wait_ge(S["evv%d" % t], 2)
+        if t < 3:
+            quant(t + 1, h, LEAVES + (t - 1) * NODES, NODES, S["qn%d" % t])
+            V.wait_ge(S["qn%d" % t], 1)
+            pick_far(pick_codes, t + 1, S["paq%d" % (t + 1)])
+            pick_one(pick_codes, t + 1, S["pbq%d" % (t + 1)])
+        if t == 1:
+            quant(3, h, LEAVES, NODES, S.own3)
+            keep(pick_codes, runs, 2, S.kq3)
+            quant(4, h, LEAVES, NODES, S.own4)
+            V.wait_ge(S.ldv, 16)
+            V.quantize_mx(T.vq[:], T.vs[:], T.vt[:]).then_inc(S.qv, 1)
+        if t == 2:
+            quant(4, h, LEAVES + NODES, NODES, S.own4)
+            keep(pick_codes, runs2, 3, S.kq4)
+        if t == 3:
+            V.quantize_mx(T.hq[:], T.hs[:], h[:]).then_inc(S.qh, 1)
+            V.wait_ge(S.mmy, 1)
+            V.tensor_copy(T.ys[:], T.psb[:, 0:NODES]).then_inc(S.evy, 1)
+
+    A.wait_ge(S.so1, CUT)
+    A.wait_ge(S.qx1, 1)
+    pick_far(pick_scales, 1, S.pas1)
+    A.wait_ge(S.so1b, len(one))
+    pick_one(pick_scales, 1, S.pbs1)
+    for t in (1, 2, 3):
+        ready(A, t)
+        A.wait_ge(S["ars%d" % t], NS)
+        pick_scales("l%d" % t, 0, NODES, t + 1, T.lo, KIDS * (t - 1), KIDS * t, S["pls%d" % t])
+        pick_scales("r%d" % t, 0, NODES, t + 1, T.ro, KIDS * (t - 1), KIDS * t, S["prs%d" % t])
+        h = T["h%d" % t]
+        for i in (0, 2):
+            A.wait_ge(S["mm%d_%d" % (t, i)], 1)
+            A.activation(h[:, i:4 * NODES:4], bank(t, i), RELU, scale=0.05).then_inc(S["evs%d" % t], 1)
+        if t < 3:
+            A.wait_ge(S["qn%d" % t], 1)
+            pick_far(pick_scales, t + 1, S["pas%d" % (t + 1)])
+            pick_one(pick_scales, t + 1, S["pbs%d" % (t + 1)])
+        if t == 1:
+            keep(pick_scales, runs, 2, S.ks3)
+        if t == 2:
+            keep(pick_scales, runs2, 3, S.ks4)
+
+    E.wait_ge(S.qwl, 1)
+    for t in (1, 2, 3):
+        E.wait_ge(S["plq%d" % t], 1)
+        E.wait_ge(S["pls%d" % t], 1)
+        for i in range(4):
+            E.matmul_mx(bank(t, i), T.wlq[:, 128 * i:128 * i + 128], T.wls[:, 128 * i:128 * i + 128],
+                        T["l%dq" % t][:], T["l%ds" % t][:], True, False)
+        if t == 1:
+            E.wait_ge(S.qwr, 1)
+        E.wait_ge(S["prq%d" % t], 1)
+        E.wait_ge(S["prs%d" % t], 1)
+        for i in range(4):
+            E.matmul_mx(bank(t, i), T.wrq[:, 128 * i:128 * i + 128], T.wrs[:, 128 * i:128 * i + 128],
+                        T["r%dq" % t][:], T["r%ds" % t][:], False, True).then_inc(S["mm%d_%d" % (t, i)], 1)
+    E.wait_ge(S.qv, 1)
+    E.wait_ge(S.qh, 1)
+    E.matmul_mx(T.psb[:, 0:NODES], T.vq[:], T.vs[:], T.hq[:], T.hs[:], True, True).then_inc(S.mmy, 1)
+
+    g.iota(T.pi[:], [[0, KEPT]], 0, 1).then_inc(S.iot, 1)
+    g.iota(T.ci[:], [[16, KEPT]], BASE, 0).then_inc(S.iot, 1)
+    left = 0
+    for t in (1, 2, 3):
+        for form, pick, sends in plan(topo, cores, rank):
+            trs = []
+            for d, k, es in sends:
+                rid, pid, _se = topo.addr(cores[d])
+                at = BASE + ((t - 1) * N + rank) * CAPP
+                src = T["o%d%s" % (t, form)][:, CAPP * k:CAPP * k + CAPP]
+                dst = T["w%d%s" % (t + 1, form)][:, at:at + CAPP]
+                if form == "q":
+                    src, dst = src.bitcast(dt.uint8), dst.bitcast(dt.uint8)
+                left += len(es)
+                trs.append(RemoteDMATransfer(dst_ids=[DstId(rid=rid, pnc=pid)], dma_engine_mask=bits(es),
+                                             remote_sem=S["ar%s%d" % (form, t)], src=src, dst=dst))
+            g.wait_ge(S["%s%s%d" % (pick, form, t)], 1)
+            g.remote_dma_fused(trs, local_sem=S.left)
+    g.wait_ge(S.left, left)
+
+    Y.wait_ge(S.evy, 1)
+    Y.dma_start(T.y[:], T.ys[:]).then_inc(S.sty, 16)
+    Y.wait_ge(S.sty, 16)

@@ -7,24 +7,52 @@ SENT = (N - 1) * CAPP
 F8 = "float8_e4m3fn_x4"
 KIDS = NODES // 16
 OFFS = SENT // 16
-KEPT = 2 * N * CAPP // 16
+LEAST = 128
+TILE = SENT + NODES
+EARLY = 64
+CUTS = [(0, SENT), (SENT, TILE)]
+WIDE = {1: LEAVES, 2: BASE + N * CAPP, 3: BASE + 2 * N * CAPP, 4: BASE + 3 * N * CAPP}
+
+
+def first(t):
+    return LEAVES + (t - 1) * NODES
+
 
 SCRATCH = {
     "xt": ("sbuf", [128, 4 * LEAVES], "bfloat16"),
     "wlt": ("sbuf", [128, 2048], "bfloat16"),
     "wrt": ("sbuf", [128, 2048], "bfloat16"),
     "vt": ("sbuf", [128, 512], "bfloat16"),
-    "sni": ("sbuf", [128, LEVELS * N * 2], "int32"),
-    "lci": ("sbuf", [128, LEVELS * KIDS], "int32"),
-    "rci": ("sbuf", [128, LEVELS * KIDS], "int32"),
-    "pi": ("sbuf", [128, KEPT], "int32"),
-    "pm": ("sbuf", [128, KEPT], "int32"),
-    "ci": ("sbuf", [128, KEPT], "int32"),
-    "ki": ("sbuf", [128, KEPT], "int32"),
-    "ko": ("sbuf", [128, KEPT], "uint16"),
-    "so": ("sbuf", [128, LEVELS * OFFS], "uint16"),
-    "lo": ("sbuf", [128, LEVELS * KIDS], "uint16"),
-    "ro": ("sbuf", [128, LEVELS * KIDS], "uint16"),
+    "sni": ("sbuf", [128, LEVELS, N, 2], "int32"),
+    "kid": ("sbuf", [128, 2, LEVELS * KIDS], "int32"),
+    "sl": ("sbuf", [128, LEVELS, OFFS], "uint16"),
+    "sm": ("sbuf", [128, 2, OFFS], "uint16"),
+    "lr": ("sbuf", [128, 2, LEVELS, OFFS + KIDS], "uint16"),
+    "lrf": ("sbuf", [128, 2, LEVELS, OFFS + KIDS], "float32"),
+    "pi": ("sbuf", [128, 2 * OFFS], "int32"),
+    "ev": ("sbuf", [128, KIDS], "int32"),
+    "jj": ("sbuf", [128, 2 * OFFS], "int32"),
+    "pm": ("sbuf", [128, 2 * OFFS], "int32"),
+    "b4": ("sbuf", [128, KIDS], "int32"),
+    "pa": ("sbuf", [128, 1], "int32"),
+    "s1": ("sbuf", [128, 1], "int32"),
+    "cbi": ("sbuf", [128, KIDS], "int32"),
+    "cb": ("sbuf", [128, KIDS], "uint16"),
+    "co": ("sbuf", [128, 2], "uint16"),
+    "jf": ("sbuf", [128, 2 * OFFS], "float32"),
+    "pkw": ("sbuf", [128, KIDS], "float32"),
+    "ii": ("sbuf", [128, 2 * OFFS], "float32"),
+    "off": ("sbuf", [128, 16], "uint16"),
+    "bb": ("sbuf", [128, NODES], "float32"),
+    "ff": ("sbuf", [128, NODES], "float32"),
+    "gg": ("sbuf", [128, SENT], "float32"),
+    "gt": ("sbuf", [128, SENT], "float32"),
+    "r1": ("sbuf", [128, 2 * OFFS], "float32"),
+    "r2": ("sbuf", [128, 2 * OFFS], "float32"),
+    "d0": ("sbuf", [128, 4 * OFFS], "float32"),
+    "d1": ("sbuf", [128, 64], "float32"),
+    "sc": ("sbuf", [128, 4 * OFFS], "float32"),
+    "n0": ("sbuf", [128, 1], "float32"),
     "wlq": ("sbuf", [128, 512], F8), "wls": ("sbuf", [128, 512], "uint8"),
     "wrq": ("sbuf", [128, 512], F8), "wrs": ("sbuf", [128, 512], "uint8"),
     "vq": ("sbuf", [128, 128], F8), "vs": ("sbuf", [128, 128], "uint8"),
@@ -33,47 +61,46 @@ SCRATCH = {
     "psa": ("psum", [128, 2048], "float32"),
     "psb": ("psum", [128, 2048], "float32"),
 }
-WIDE = {1: LEAVES, 2: BASE + N * CAPP, 3: BASE + 2 * N * CAPP, 4: BASE + 3 * N * CAPP}
 for _t in WIDE:
-    SCRATCH["w%dq" % _t] = ("sbuf", [128, WIDE[_t]], F8)
-    SCRATCH["w%ds" % _t] = ("sbuf", [128, WIDE[_t]], "uint8")
+    SCRATCH["w%dq" % _t] = ("sbuf", [128, WIDE[_t] + LEAST], F8)
+    SCRATCH["w%ds" % _t] = ("sbuf", [128, WIDE[_t] + LEAST], "uint8")
 for _t in (1, 2, 3):
     SCRATCH["o%dq" % _t] = ("sbuf", [128, SENT], F8)
     SCRATCH["o%ds" % _t] = ("sbuf", [128, SENT], "uint8")
-    SCRATCH["h%d" % _t] = ("sbuf", [128, 4 * NODES], "bfloat16")
+    SCRATCH["h%d" % _t] = ("sbuf", [128, 4 * TILE], "bfloat16")
     for _n in ("l", "r"):
-        SCRATCH["%s%dq" % (_n, _t)] = ("sbuf", [128, NODES], F8)
-        SCRATCH["%s%ds" % (_n, _t)] = ("sbuf", [128, NODES], "uint8")
+        SCRATCH["%s%dq" % (_n, _t)] = ("sbuf", [128, TILE], F8)
+        SCRATCH["%s%ds" % (_n, _t)] = ("sbuf", [128, TILE], "uint8")
 
-SEMAPHORES = ["ldx", "ldsn", "ldwl", "ldwr", "ldv", "ldlc", "ldrc", "so1", "so1b", "so23", "clo", "cro",
-              "iot", "iom", "ioa", "cko",
-              "qx1", "qx2", "qx34", "qwl", "qwr", "qv", "own3", "own4", "kq3", "ks3", "kq4", "ks4", "left",
-              "qh", "mmy", "evy", "sty"]
+SEMAPHORES = ["ldx", "ldsn", "ldwl", "ldwr", "ldwr2", "ldv", "ldk", "so1", "so2", "so3", "iot", "k1", "k2", "k3",
+              "nat", "win", "a1", "a2", "new", "dof", "ab", "t1", "ag", "t2", "d5", "d6", "d7", "m1", "m2", "m3", "dsm",
+              "qx1", "qx2", "qwl", "qwr", "qwr2", "qv", "c3", "c4", "left", "qh", "mmy", "evy", "sty"]
 for _t in (1, 2, 3):
-    SEMAPHORES += ["%s%d" % (_n, _t) for _n in ("paq", "pas", "pbq", "pbs", "arq", "ars", "plq", "pls", "prq", "prs",
-                                                "evv", "evs", "qn")]
-    SEMAPHORES += ["mm%d_%d" % (_t, _i) for _i in range(4)]
+    SEMAPHORES += ["%s%d" % (_n, _t) for _n in ("paq", "pas", "pbq", "pbs", "pcq", "pcs", "arq", "ars")]
+    for _b in range(3 if _t < 3 else 1):
+        SEMAPHORES += ["%s%d_%d" % (_n, _t, _b) for _n in ("pl", "pr", "ev", "qn", "m0", "m1", "m2", "m3")]
 
 
 def order(topo, cores, s):
     me = topo.chip(cores[s])
     far, near, mate = [], [], []
-    for k in range(1, N):
-        d = (s + k) % N
+    for d in range(N):
+        if d == s:
+            continue
         c = topo.chip(cores[d])
         (mate if topo.mates(me, c) else near if topo.same_plane(me, c) else far).append(d)
-    return far, near + mate
+    return far, near, mate
 
 
 def plan(topo, cores, s):
-    far, one = order(topo, cores, s)
-    e = topo.engines(cores[s], cores[far[0]])[:8]
-    a = [(d, k, e[4 * k:4 * k + 4]) for k, d in enumerate(far)]
-
-    def others(big, small):
-        return [(d, len(far) + k, es) for k, (d, es) in enumerate(zip(one, (big, small[:2], small[2:])))]
-    return [("q", "pa", a), ("s", "pa", a),
-            ("q", "pb", others(e[0::2], e[1::2])), ("s", "pb", others(e[1::2], e[0::2]))]
+    groups = order(topo, cores, s)
+    e = topo.engines(cores[s], cores[groups[0][0]])
+    calls, k = {}, 0
+    for name, ds in zip("abc", groups):
+        share = len(e) // len(ds)
+        calls[name] = [(d, k + j, e[share * j:share * j + share]) for j, d in enumerate(ds)]
+        k += len(ds)
+    return [(form, "pa" if name == "a" else "pb", calls[name]) for form, name in ("qa", "sa", "qb", "sb", "qc", "sc")]
 
 
 def bits(es):
@@ -91,182 +118,269 @@ def rank_program(g, core, T, topo):
     S = T.sem
     V, A, E, Y = g.vector, g.scalar, g.tensor, g.sync
     RELU, COPY = ActivationFunctionType.Relu, ActivationFunctionType.Copy
+    OP, FN = AluOpType, ActivationFunctionType
 
     def arrivals(form):
         return sum(len(es) for s in range(N) if s != rank for f, _p, trs in plan(topo, cores, s) if f == form
                    for d, _k, es in trs if d == rank)
     NQ, NS = arrivals("q"), arrivals("s")
+    far, near, mate = order(topo, cores, rank)
+    GROUPS = {"a": (0, len(far)), "b": (len(far), N - 1)}
 
-    def runs_of(levels):
-        cuts = [-1] + [N * t + rank for t in range(levels)] + [N * levels]
-        return [(a + 1, b) for a, b in zip(cuts, cuts[1:]) if b > a + 1]
-    runs, runs2 = runs_of(1), runs_of(2)
-    far, one = order(topo, cores, rank)
-    CUT = len(far)
+    def slot_runs(t):
+        at = BASE + (t - 1) * N * CAPP
+        return [(at + a * CAPP, at + b * CAPP) for a, b in ((0, rank), (rank + 1, N)) if b > a]
+
+    def batches(t):
+        return [(a, b, min(a, b - LEAST)) for a, b in (CUTS if t < 3 else [(SENT, TILE)])]
 
     def table(q, out, src, groups, sem):
         for k in groups:
-            q.dma_start(out[16 * k:16 * k + 16, :], src[:, :]).then_inc(sem, 16)
+            q.dma_start(out(slice(16 * k, 16 * k + 16)), src[:, :]).then_inc(sem, 16)
     Y.dma_start(T.xt[:], T.x[:]).then_inc(S.ldx, 16)
-    table(A, T.sni, T.sn, range(0, 5), S.ldsn)
-    table(Y, T.sni, T.sn, range(5, 8), S.ldsn)
-    Y.dma_start(T.wlt[:], T.wl[:]).then_inc(S.ldwl, 16)
-    A.dma_start(T.wrt[:], T.wr[:]).then_inc(S.ldwr, 16)
-    table(Y, T.lci, T.lc, range(8), S.ldlc)
-    table(A, T.rci, T.rc, range(8), S.ldrc)
+    table(A, lambda p: T.sni[p], T.sn, range(0, 3), S.ldsn)
+    table(Y, lambda p: T.sni[p], T.sn, range(3, 4), S.ldsn)
+    table(Y, lambda p: T.kid[p, 0], T.lc, range(2), S.ldk)
+    table(A, lambda p: T.kid[p, 1], T.rc, range(2), S.ldk)
+    Y.dma_start(T.wlt[:, 0:1024], T.wl[:, 0:1024]).then_inc(S.ldwl, 16)
+    A.dma_start(T.wlt[:, 1024:2048], T.wl[:, 1024:2048]).then_inc(S.ldwl, 16)
+    Y.dma_start(T.wrt[:, 0:1024], T.wr[:, 0:1024]).then_inc(S.ldwr, 16)
+    Y.dma_start(T.wrt[:, 1024:2048], T.wr[:, 1024:2048]).then_inc(S.ldwr2, 16)
+
+    def carry(t, u, runs, sem):
+        for a, b in runs:
+            Y.dma_start(T["w%dq" % u][:, a:b].bitcast(dt.uint8), T["w%dq" % t][:, a:b].bitcast(dt.uint8)).then_inc(sem, 16)
+            Y.dma_start(T["w%ds" % u][:, a:b], T["w%ds" % t][:, a:b]).then_inc(sem, 16)
+        return 32 * len(runs)
+    Y.wait_ge(S.qx2, 1)
+    Y.wait_ge(S.arq1, NQ)
+    Y.wait_ge(S.ars1, NS)
+    C3 = carry(2, 3, slot_runs(1) + [(0, LEAVES)], S.c3)
+    C4 = carry(2, 4, slot_runs(1) + [(0, LEAVES)], S.c4)
+    Y.wait_ge(S.qn1_1, 1)
+    Y.wait_ge(S.arq2, NQ)
+    Y.wait_ge(S.ars2, NS)
+    C4 += carry(3, 4, slot_runs(2) + [(first(1), first(2))], S.c4)
     Y.dma_start(T.vt[:], T.v[:]).then_inc(S.ldv, 16)
 
-    def slots_list(t, ds, k, sem):
-        for d in ds:
-            at, of = OFFS * (t - 1) + 2 * k, 2 * (N * (t - 1) + d)
-            V.tensor_copy(T.so[:, at:at + 2], T.sni[:, of:of + 2]).then_inc(sem, 1)
-            k += 1
+    HALVES = (slice(0, 64), slice(64, 128))
+    QUARTERS = [slice(32 * a, 32 * a + 32) for a in range(4)]
 
-    def quant(t, tile, at, n, sem):
-        V.quantize_mx(T["w%dq" % t][:, at:at + n], T["w%ds" % t][:, at:at + n], tile[:]).then_inc(sem, 1)
+    def slots_list(ds, k, sem):
+        step = ds[-1] - ds[0] or 1
+        for half in HALVES:
+            V.tensor_copy(T.sl[half, :, 2 * k:2 * (k + len(ds))],
+                          T.sni[0:64, :, ds[0]:ds[-1] + 1:step, :]).then_inc(sem, 1)
 
-    def pick_codes(name, at, n, t, off, a, b, sem):
-        V.tensor_copy(T[name + "q"][:, at:at + n].bitcast(dt.uint32),
-                      T["w%dq" % t][:, 0:WIDE[t]].bitcast(dt.uint32).indirect(off[:, a:b])).then_inc(sem, 1)
+    def pick(q, out, at, n, t, wide, off, sem):
+        if q is V:
+            V.tensor_copy(T[out + "q"][:, at:at + n].bitcast(dt.uint32),
+                          T["w%dq" % t][:, 0:wide].bitcast(dt.uint32).indirect(off)).then_inc(sem, 1)
+        else:
+            A.activation(T[out + "s"][:, at:at + n], T["w%ds" % t][:, 0:wide].indirect(off), COPY).then_inc(sem, 1)
 
-    def pick_scales(name, at, n, t, off, a, b, sem):
-        A.activation(T[name + "s"][:, at:at + n], T["w%ds" % t][:, 0:WIDE[t]].indirect(off[:, a:b]), COPY).then_inc(sem, 1)
+    def pick_slots(q, t, name):
+        a, b = GROUPS[name]
+        off = T.sl[:, 0, 2 * a:2 * b] if t == 1 else T.sm[:, t - 2, 2 * a:2 * b]
+        pick(q, "o%d" % t, a * CAPP, (b - a) * CAPP, t, WIDE[t], off, S["p%s%s%d" % (name, "q" if q is V else "s", t)])
 
-    def pick_far(pick, t, sem):
-        pick("o%d" % t, 0, CUT * CAPP, t, T.so, OFFS * (t - 1), OFFS * (t - 1) + 2 * CUT, sem)
+    def pick_kids(q, t, b, side):
+        a, z, _m = batches(t)[b]
+        pick(q, "%s%d" % ("lr"[side], t), a, z - a, t + 1, WIDE[t + 1], T.lr[:, side, t - 1, a // 16:z // 16],
+             S["p%s%d_%d" % ("lr"[side], t, b)])
 
-    def pick_one(pick, t, sem):
-        pick("o%d" % t, CUT * CAPP, SENT - CUT * CAPP, t, T.so, OFFS * (t - 1) + 2 * CUT, OFFS * t, sem)
+    def banks(t, b):
+        return T.psa if b == 0 else T.psb
 
-    def keep(pick, rs, t, sem):
-        for a, b in rs:
-            pick("w%d" % (t + 1), BASE + a * CAPP, (b - a) * CAPP, t, T.ko, 2 * a, 2 * b, sem)
+    def evict(q, t, b, i):
+        a, z, m = batches(t)[b]
+        src, out = banks(t, b)[:, 512 * i + a - m:512 * i + z - m], T["h%d" % t][:, 4 * a + i:4 * z:4]
+        q.wait_ge(S["m%d%d_%d" % (i, t, b)], 1)
+        if q is V:
+            V.tensor_scalar(out, src, 0.0, 0.05, OP.max, OP.mult).then_inc(S["ev%d_%d" % (t, b)], 1)
+        else:
+            A.activation(out, src, RELU, scale=0.05).then_inc(S["ev%d_%d" % (t, b)], 1)
 
-    def bank(t, i):
-        return (T.psa if t % 2 else T.psb)[:, 512 * i:512 * i + NODES]
+    def quant(name, at, tile, a, z, sem):
+        V.quantize_mx(T[name + "q"][:, at:at + z - a], T[name + "s"][:, at:at + z - a], tile[:, 4 * a:4 * z]).then_inc(sem, 1)
 
-    V.wait_ge(S.iot, 2)
-    V.tensor_scalar(T.pm[:], T.pi[:], 15, None, AluOpType.bitwise_and).then_inc(S.iom, 1)
-    V.wait_ge(S.iom, 1)
-    V.tensor_tensor(T.ki[:], T.pm[:], T.ci[:], AluOpType.add).then_inc(S.ioa, 1)
-    V.wait_ge(S.ioa, 1)
-    V.tensor_copy(T.ko[:], T.ki[:]).then_inc(S.cko, 1)
+    V.memset(T.lr[0:32], 0).then_inc(S.k1, 1)
+    V.memset(T.d0[:], 0.0).then_inc(S.k1, 1)
+    V.memset(T.d1[:], 0.0).then_inc(S.k1, 1)
+    for k, half in enumerate(HALVES):
+        V.memset(T.n0[half, :], float(first(k + 1))).then_inc(S.k1, 1)
+    V.wait_ge(S.iot, 3)
+    V.tensor_scalar(T.b4[:], T.pi[:, 0:KIDS], 4, 1, OP.logical_shift_right, OP.bitwise_and).then_inc(S.k1, 1)
+    V.tensor_scalar(T.pa[:], T.pi[:, 0:1], 14, None, OP.bitwise_and).then_inc(S.k1, 1)
+    V.tensor_scalar(T.pm[:], T.pi[:], 15, None, OP.bitwise_and).then_inc(S.k1, 1)
+    V.wait_ge(S.k1, 8)
+    V.tensor_tensor(T.cbi[:], T.ev[:], T.b4[:], OP.add).then_inc(S.k2, 1)
+    V.tensor_tensor(T.s1[:], T.pa[:], T.b4[:, 0:1], OP.add).then_inc(S.k2, 1)
+    V.tensor_tensor(T.jf[:], T.jj[:], T.pm[:], OP.add).then_inc(S.k2, 1)
+    V.wait_ge(S.k2, 3)
+    V.tensor_copy(T.cb[:], T.cbi[:]).then_inc(S.k3, 1)
+    for k, half in enumerate(HALVES):
+        V.tensor_scalar(T.co[half, 0:1], T.s1[half, :], 2, 2 * OFFS * k + 1, OP.mult, OP.add).then_inc(S.k3, 1)
 
-    V.wait_ge(S.ldsn, 128)
-    slots_list(1, far, 0, S.so1)
+    V.wait_ge(S.ldsn, 64)
+    slots_list(far, GROUPS["a"][0], S.so1)
     V.wait_ge(S.ldx, 16)
-    quant(1, T.xt, 0, LEAVES, S.qx1)
-    V.wait_ge(S.so1, CUT)
+    quant("w1", 0, T.xt, 0, LEAVES, S.qx1)
+    V.wait_ge(S.so1, 2)
     V.wait_ge(S.qx1, 1)
-    pick_far(pick_codes, 1, S.paq1)
-    slots_list(1, one, CUT, S.so1b)
-    V.wait_ge(S.so1b, len(one))
-    pick_one(pick_codes, 1, S.pbq1)
-    quant(2, T.xt, 0, LEAVES, S.qx2)
-    quant(3, T.xt, 0, LEAVES, S.qx34)
-    quant(4, T.xt, 0, LEAVES, S.qx34)
-    for t in (2, 3):
-        slots_list(t, far + one, 0, S.so23)
-    V.wait_ge(S.ldwl, 16)
-    V.quantize_mx(T.wlq[:], T.wls[:], T.wlt[:]).then_inc(S.qwl, 1)
+    pick_slots(V, 1, "a")
+    V.wait_ge(S.ldk, 64)
+    for a, part in enumerate(QUARTERS):
+        V.tensor_copy(T.pkw[part, :], T.kid[0:32, a % 2, KIDS * (a // 2):KIDS * (a // 2 + 1)]).then_inc(S.win, 1)
+    slots_list(near, len(far), S.so2)
+    slots_list(mate, len(far + near), S.so2)
+    V.wait_ge(S.so2, 4)
+    pick_slots(V, 1, "b")
+
+    ODD, EVEN = slice(1, 4 * OFFS, 2), slice(0, 4 * OFFS, 2)
+    V.wait_ge(S.k3, 3)
+    V.tensor_copy(T.d1[:, ODD], T.sl[:, 1:3, :]).then_inc(S.m1, 1)
+    V.wait_ge(S.ab, 1)
+    V.transpose(T.ff[:], T.bb[:]).then_inc(S.t1, 1)
+    V.wait_ge(S.m1, 1)
+    V.tensor_scalar(T.off[:], T.d1[:].indirect(T.co[:, 0:1]), T.n0[:], float(NODES - 1), OP.subtract, OP.min).then_inc(S.dof, 1)
+    V.tensor_copy(T.lr[0:32, :, :, OFFS:], T.kid[0:32]).then_inc(S.d5, 1)
+    quant("w2", 0, T.xt, 0, LEAVES, S.qx2)
+    V.wait_ge(S.dof, 1)
+    V.tensor_tensor(T.d1[:, EVEN], T.jf[:], T.d1[:, ODD], OP.subtract).then_inc(S.m2, 1)
+    V.wait_ge(S.ldwl, 32)
+    quant("wl", 0, T.wlt, 0, 512, S.qwl)
+    V.wait_ge(S.ag, 1)
+    V.transpose(T.gt[:], T.gg[:]).then_inc(S.t2, 1)
+    V.wait_ge(S.m2, 1)
+    V.wait_ge(S.new, 1)
+    V.tensor_tensor_scan(T.sc[:], T.d0[:], T.d1[:, 0:4 * OFFS], 0.0, OP.mult, OP.add).then_inc(S.m3, 1)
+    V.wait_ge(S.t2, 1)
+    for a, part in enumerate(QUARTERS):
+        V.tensor_copy(T.lr[0:32, a % 2, a // 2, 0:OFFS], T.gt[part, 0:SENT:16]).then_inc(S.d5, 1)
+    V.wait_ge(S.d5, 5)
+    V.tensor_copy(T.lr[32:64], T.lr[0:32]).then_inc(S.d6, 1)
+    V.wait_ge(S.m3, 1)
+    V.tensor_copy(T.sm[:], T.sc[:, ODD]).then_inc(S.dsm, 1)
     V.wait_ge(S.ldwr, 16)
-    V.quantize_mx(T.wrq[:], T.wrs[:], T.wrt[:]).then_inc(S.qwr, 1)
-    V.wait_ge(S.ldlc, 128)
-    V.tensor_copy(T.lo[:], T.lci[:]).then_inc(S.clo, 1)
-    V.wait_ge(S.ldrc, 128)
-    V.tensor_copy(T.ro[:], T.rci[:]).then_inc(S.cro, 1)
+    quant("wr", 0, T.wrt, 0, 256, S.qwr)
+    V.wait_ge(S.d6, 1)
+    V.tensor_copy(T.lr[64:128], T.lr[0:64]).then_inc(S.d7, 1)
 
     def ready(q, t):
         if t == 1:
             q.wait_ge(S.qx2, 1)
-            q.wait_ge(S.qx34, 2)
-            q.wait_ge(S.so23, 2 * (N - 1))
-            q.wait_ge(S.clo, 1)
-            q.wait_ge(S.cro, 1)
-            q.wait_ge(S.cko, 1)
+            q.wait_ge(S.d7, 1)
+            q.wait_ge(S.dsm, 1)
         if t == 2:
-            q.wait_ge(S.own3, 1)
-            q.wait_ge(S.kq3 if q is V else S.ks3, len(runs))
+            q.wait_ge(S.qn1_1, 1)
+            q.wait_ge(S.c3, C3)
         if t == 3:
-            q.wait_ge(S.own4, 2)
-            q.wait_ge(S.kq4 if q is V else S.ks4, len(runs2))
+            q.wait_ge(S.qn2_1, 1)
+            q.wait_ge(S.c4, C4)
 
-    for t in (1, 2, 3):
+    for t in (1, 2):
+        h, w = T["h%d" % t], "w%d" % (t + 1)
         ready(V, t)
         V.wait_ge(S["arq%d" % t], NQ)
-        pick_codes("l%d" % t, 0, NODES, t + 1, T.lo, KIDS * (t - 1), KIDS * t, S["plq%d" % t])
-        pick_codes("r%d" % t, 0, NODES, t + 1, T.ro, KIDS * (t - 1), KIDS * t, S["prq%d" % t])
-        h = T["h%d" % t]
-        for i in (1, 3):
-            V.wait_ge(S["mm%d_%d" % (t, i)], 1)
-            V.tensor_scalar(h[:, i:4 * NODES:4], bank(t, i), 0.0, 0.05, AluOpType.max, AluOpType.mult).then_inc(S["evv%d" % t], 1)
-        V.wait_ge(S["evs%d" % t], 2)
-        V.wait_ge(S["evv%d" % t], 2)
-        if t < 3:
-            quant(t + 1, h, LEAVES + (t - 1) * NODES, NODES, S["qn%d" % t])
-            V.wait_ge(S["qn%d" % t], 1)
-            pick_far(pick_codes, t + 1, S["paq%d" % (t + 1)])
-            pick_one(pick_codes, t + 1, S["pbq%d" % (t + 1)])
+        pick_kids(V, t, 0, 0)
+        pick_kids(V, t, 0, 1)
         if t == 1:
-            quant(3, h, LEAVES, NODES, S.own3)
-            keep(pick_codes, runs, 2, S.kq3)
-            quant(4, h, LEAVES, NODES, S.own4)
-            V.wait_ge(S.ldv, 16)
-            V.quantize_mx(T.vq[:], T.vs[:], T.vt[:]).then_inc(S.qv, 1)
-        if t == 2:
-            quant(4, h, LEAVES + NODES, NODES, S.own4)
-            keep(pick_codes, runs2, 3, S.kq4)
-        if t == 3:
-            V.quantize_mx(T.hq[:], T.hs[:], h[:]).then_inc(S.qh, 1)
-            V.wait_ge(S.mmy, 1)
-            V.tensor_copy(T.ys[:], T.psb[:, 0:NODES]).then_inc(S.evy, 1)
+            V.wait_ge(S.ldwr2, 16)
+            quant("wr", 256, T.wrt, 256, 512, S.qwr2)
+        pick_kids(V, t, 1, 0)
+        for i in (1, 3):
+            evict(V, t, 0, i)
+        V.wait_ge(S["pl%d_1" % t], 2)
+        V.wait_ge(S["ev%d_0" % t], 4)
+        quant(w, first(t), h, 0, SENT, S["qn%d_0" % t])
+        V.wait_ge(S["qn%d_0" % t], 1)
+        pick_slots(V, t + 1, "a")
+        pick_slots(V, t + 1, "b")
+        pick_kids(V, t, 1, 1)
+        for i in (1, 3):
+            evict(V, t, 1, i)
+        V.wait_ge(S["ev%d_1" % t], 4)
+        quant("w%d" % (t + 2), first(t), h, SENT, TILE, S["qn%d_1" % t])
+    ready(V, 3)
+    V.wait_ge(S.arq3, NQ)
+    pick_kids(V, 3, 0, 0)
+    pick_kids(V, 3, 0, 1)
+    V.wait_ge(S.ldv, 16)
+    quant("v", 0, T.vt, 0, 128, S.qv)
+    for i in (1, 3):
+        evict(V, 3, 0, i)
+    V.wait_ge(S.ev3_0, 4)
+    quant("h", 0, T.h3, SENT, TILE, S.qh)
+    V.wait_ge(S.mmy, 1)
+    V.tensor_copy(T.ys[:], T.psb[:, 0:NODES]).then_inc(S.evy, 1)
 
-    A.wait_ge(S.so1, CUT)
+    A.wait_ge(S.so1, 2)
     A.wait_ge(S.qx1, 1)
-    pick_far(pick_scales, 1, S.pas1)
-    A.wait_ge(S.so1b, len(one))
-    pick_one(pick_scales, 1, S.pbs1)
-    for t in (1, 2, 3):
+    pick_slots(A, 1, "a")
+    A.wait_ge(S.win, 4)
+    A.wait_ge(S.k3, 3)
+    A.activation(T.bb[:], T.pkw[:].indirect(T.cb[:]), COPY).then_inc(S.ab, 1)
+    A.wait_ge(S.so2, 4)
+    pick_slots(A, 1, "b")
+    A.wait_ge(S.m1, 1)
+    for t in (1, 2):
+        A.activation(T.r1[:, OFFS * (t - 1):OFFS * t], T.d1[:, 2 * OFFS * (t - 1) + 1:2 * OFFS * t:2], FN.Abs,
+                     bias=-(first(t) + (NODES - 1) / 2)).then_inc(S.a1, 1)
+    A.wait_ge(S.t1, 1)
+    A.wait_ge(S.dof, 1)
+    A.activation(T.gg[:], T.ff[:].indirect(T.off[:, 0:OFFS]), COPY).then_inc(S.ag, 1)
+    A.wait_ge(S.a1, 2)
+    A.activation(T.r2[:], T.r1[:], FN.Sign, bias=NODES / 2, scale=-1.0).then_inc(S.a2, 1)
+    A.wait_ge(S.a2, 1)
+    A.activation(T.d0[:, ODD], T.r2[:], RELU).then_inc(S.new, 1)
+    for t in (1, 2):
         ready(A, t)
         A.wait_ge(S["ars%d" % t], NS)
-        pick_scales("l%d" % t, 0, NODES, t + 1, T.lo, KIDS * (t - 1), KIDS * t, S["pls%d" % t])
-        pick_scales("r%d" % t, 0, NODES, t + 1, T.ro, KIDS * (t - 1), KIDS * t, S["prs%d" % t])
-        h = T["h%d" % t]
+        pick_kids(A, t, 0, 0)
+        pick_kids(A, t, 0, 1)
+        pick_kids(A, t, 1, 0)
         for i in (0, 2):
-            A.wait_ge(S["mm%d_%d" % (t, i)], 1)
-            A.activation(h[:, i:4 * NODES:4], bank(t, i), RELU, scale=0.05).then_inc(S["evs%d" % t], 1)
-        if t < 3:
-            A.wait_ge(S["qn%d" % t], 1)
-            pick_far(pick_scales, t + 1, S["pas%d" % (t + 1)])
-            pick_one(pick_scales, t + 1, S["pbs%d" % (t + 1)])
-        if t == 1:
-            keep(pick_scales, runs, 2, S.ks3)
-        if t == 2:
-            keep(pick_scales, runs2, 3, S.ks4)
+            evict(A, t, 0, i)
+        A.wait_ge(S["qn%d_0" % t], 1)
+        pick_slots(A, t + 1, "a")
+        pick_slots(A, t + 1, "b")
+        pick_kids(A, t, 1, 1)
+        for i in (0, 2):
+            evict(A, t, 1, i)
+    ready(A, 3)
+    A.wait_ge(S.ars3, NS)
+    pick_kids(A, 3, 0, 0)
+    pick_kids(A, 3, 0, 1)
+    for i in (0, 2):
+        evict(A, 3, 0, i)
 
     E.wait_ge(S.qwl, 1)
     for t in (1, 2, 3):
-        E.wait_ge(S["plq%d" % t], 1)
-        E.wait_ge(S["pls%d" % t], 1)
-        for i in range(4):
-            E.matmul_mx(bank(t, i), T.wlq[:, 128 * i:128 * i + 128], T.wls[:, 128 * i:128 * i + 128],
-                        T["l%dq" % t][:], T["l%ds" % t][:], True, False)
-        if t == 1:
-            E.wait_ge(S.qwr, 1)
-        E.wait_ge(S["prq%d" % t], 1)
-        E.wait_ge(S["prs%d" % t], 1)
-        for i in range(4):
-            E.matmul_mx(bank(t, i), T.wrq[:, 128 * i:128 * i + 128], T.wrs[:, 128 * i:128 * i + 128],
-                        T["r%dq" % t][:], T["r%ds" % t][:], False, True).then_inc(S["mm%d_%d" % (t, i)], 1)
+        for b, (_a, z, m) in enumerate(batches(t)):
+            for side, w in enumerate(("wl", "wr")):
+                if (t, b, side) == (1, 0, 1):
+                    E.wait_ge(S.qwr, 1)
+                name = "%s%d" % ("lr"[side], t)
+                E.wait_ge(S["p%s_%d" % (name, b)], 2)
+                for i in range(4):
+                    if (t, b, side, i) == (1, 0, 1, 2):
+                        E.wait_ge(S.qwr2, 1)
+                    mm = E.matmul_mx(banks(t, b)[:, 512 * i:512 * i + z - m], T[w + "q"][:, 128 * i:128 * i + 128],
+                                     T[w + "s"][:, 128 * i:128 * i + 128], T[name + "q"][:, m:z], T[name + "s"][:, m:z],
+                                     side == 0, side == 1)
+                    if side:
+                        mm.then_inc(S["m%d%d_%d" % (i, t, b)], 1)
     E.wait_ge(S.qv, 1)
     E.wait_ge(S.qh, 1)
     E.matmul_mx(T.psb[:, 0:NODES], T.vq[:], T.vs[:], T.hq[:], T.hs[:], True, True).then_inc(S.mmy, 1)
 
-    g.iota(T.pi[:], [[0, KEPT]], 0, 1).then_inc(S.iot, 1)
-    g.iota(T.ci[:], [[16, KEPT]], BASE, 0).then_inc(S.iot, 1)
+    g.iota(T.pi[:], [[0, 2 * OFFS]], 0, 1).then_inc(S.iot, 1)
+    g.iota(T.ev[:], [[2, KIDS // 2], [0, 2]], 0, 0).then_inc(S.iot, 1)
+    g.iota(T.jj[:], [[NODES, 2], [16, OFFS]], LEAVES, 0).then_inc(S.iot, 1)
     left = 0
     for t in (1, 2, 3):
-        for form, pick, sends in plan(topo, cores, rank):
+        for form, picked, sends in plan(topo, cores, rank):
             trs = []
             for d, k, es in sends:
                 rid, pid, _se = topo.addr(cores[d])
@@ -278,7 +392,7 @@ def rank_program(g, core, T, topo):
                 left += len(es)
                 trs.append(RemoteDMATransfer(dst_ids=[DstId(rid=rid, pnc=pid)], dma_engine_mask=bits(es),
                                              remote_sem=S["ar%s%d" % (form, t)], src=src, dst=dst))
-            g.wait_ge(S["%s%s%d" % (pick, form, t)], 1)
+            g.wait_ge(S["%s%s%d" % (picked, form, t)], 1)
             g.remote_dma_fused(trs, local_sem=S.left)
     g.wait_ge(S.left, left)
 

from concourse.bass import DstId, RemoteDMATransfer
from concourse.mybir import dt, AluOpType, ActivationFunctionType

N, LEAVES, NODES, CAPP, LEVELS = 6, 128, 192, 32, 3
BASE = LEAVES + LEVELS * NODES
SENT = (N - 1) * CAPP
F8 = "float8_e4m3fn_x4"
KIDS = NODES // 16
OFFS = SENT // 16
LEAST = 128
TILE = SENT + NODES
EARLY = 64
CUTS = [(0, SENT), (SENT, TILE)]
WIDE = {1: LEAVES, 2: BASE + N * CAPP, 3: BASE + 2 * N * CAPP, 4: BASE + 3 * N * CAPP}


def first(t):
    return LEAVES + (t - 1) * NODES


SCRATCH = {
    "xt": ("sbuf", [128, 4 * LEAVES], "bfloat16"),
    "wlt": ("sbuf", [128, 2048], "bfloat16"),
    "wrt": ("sbuf", [128, 2048], "bfloat16"),
    "vt": ("sbuf", [128, 512], "bfloat16"),
    "sni": ("sbuf", [128, LEVELS, N, 2], "int32"),
    "kid": ("sbuf", [128, 2, LEVELS * KIDS], "int32"),
    "sl": ("sbuf", [128, LEVELS, OFFS], "uint16"),
    "sm": ("sbuf", [128, 2, OFFS], "uint16"),
    "lr": ("sbuf", [128, 2, LEVELS, OFFS + KIDS], "uint16"),
    "lrf": ("sbuf", [128, 2, LEVELS, OFFS + KIDS], "float32"),
    "pi": ("sbuf", [128, 2 * OFFS], "int32"),
    "ev": ("sbuf", [128, KIDS], "int32"),
    "jj": ("sbuf", [128, 2 * OFFS], "int32"),
    "pm": ("sbuf", [128, 2 * OFFS], "int32"),
    "b4": ("sbuf", [128, KIDS], "int32"),
    "pa": ("sbuf", [128, 1], "int32"),
    "s1": ("sbuf", [128, 1], "int32"),
    "cbi": ("sbuf", [128, KIDS], "int32"),
    "cb": ("sbuf", [128, KIDS], "uint16"),
    "co": ("sbuf", [128, 2], "uint16"),
    "jf": ("sbuf", [128, 2 * OFFS], "float32"),
    "pkw": ("sbuf", [128, KIDS], "float32"),
    "ii": ("sbuf", [128, 2 * OFFS], "float32"),
    "off": ("sbuf", [128, 16], "uint16"),
    "bb": ("sbuf", [128, NODES], "float32"),
    "ff": ("sbuf", [128, NODES], "float32"),
    "gg": ("sbuf", [128, SENT], "float32"),
    "gt": ("sbuf", [128, SENT], "float32"),
    "r1": ("sbuf", [128, 2 * OFFS], "float32"),
    "r2": ("sbuf", [128, 2 * OFFS], "float32"),
    "d0": ("sbuf", [128, 4 * OFFS], "float32"),
    "d1": ("sbuf", [128, 64], "float32"),
    "sc": ("sbuf", [128, 4 * OFFS], "float32"),
    "n0": ("sbuf", [128, 1], "float32"),
    "wlq": ("sbuf", [128, 512], F8), "wls": ("sbuf", [128, 512], "uint8"),
    "wrq": ("sbuf", [128, 512], F8), "wrs": ("sbuf", [128, 512], "uint8"),
    "vq": ("sbuf", [128, 128], F8), "vs": ("sbuf", [128, 128], "uint8"),
    "hq": ("sbuf", [128, NODES], F8), "hs": ("sbuf", [128, NODES], "uint8"),
    "ys": ("sbuf", [128, NODES], "float32"),
    "psa": ("psum", [128, 2048], "float32"),
    "psb": ("psum", [128, 2048], "float32"),
}
for _t in WIDE:
    SCRATCH["w%dq" % _t] = ("sbuf", [128, WIDE[_t] + LEAST], F8)
    SCRATCH["w%ds" % _t] = ("sbuf", [128, WIDE[_t] + LEAST], "uint8")
for _t in (1, 2, 3):
    SCRATCH["o%dq" % _t] = ("sbuf", [128, SENT], F8)
    SCRATCH["o%ds" % _t] = ("sbuf", [128, SENT], "uint8")
    SCRATCH["h%d" % _t] = ("sbuf", [128, 4 * TILE], "bfloat16")
    for _n in ("l", "r"):
        SCRATCH["%s%dq" % (_n, _t)] = ("sbuf", [128, TILE], F8)
        SCRATCH["%s%ds" % (_n, _t)] = ("sbuf", [128, TILE], "uint8")

SEMAPHORES = ["ldx", "ldsn", "ldwl", "ldwr", "ldwr2", "ldv", "ldk", "so1", "so2", "so3", "iot", "k1", "k2", "k3",
              "nat", "win", "a1", "a2", "new", "dof", "ab", "t1", "ag", "t2", "d5", "d6", "d7", "m1", "m2", "m3", "dsm",
              "qx1", "qx2", "qwl", "qwr", "qwr2", "qv", "c3", "c4", "left", "qh", "mmy", "evy", "sty"]
for _t in (1, 2, 3):
    SEMAPHORES += ["%s%d" % (_n, _t) for _n in ("paq", "pas", "pbq", "pbs", "pcq", "pcs", "arq", "ars")]
    for _b in range(3 if _t < 3 else 1):
        SEMAPHORES += ["%s%d_%d" % (_n, _t, _b) for _n in ("pl", "pr", "ev", "qn", "m0", "m1", "m2", "m3")]


def order(topo, cores, s):
    me = topo.chip(cores[s])
    far, near, mate = [], [], []
    for d in range(N):
        if d == s:
            continue
        c = topo.chip(cores[d])
        (mate if topo.mates(me, c) else near if topo.same_plane(me, c) else far).append(d)
    return far, near, mate


def plan(topo, cores, s):
    groups = order(topo, cores, s)
    e = topo.engines(cores[s], cores[groups[0][0]])
    calls, k = {}, 0
    for name, ds in zip("abc", groups):
        share = len(e) // len(ds)
        calls[name] = [(d, k + j, e[share * j:share * j + share]) for j, d in enumerate(ds)]
        k += len(ds)
    return [(form, "pa" if name == "a" else "pb", calls[name]) for form, name in ("qa", "sa", "qb", "sb", "qc", "sc")]


def bits(es):
    m = 0
    for e in es:
        m |= 1 << e
    return m


def rank_program(g, core, T, topo):
    rank = T.rank_of(core)
    if rank is None:
        return
    cores = list(T.cores)
    S = T.sem
    V, A, E, Y = g.vector, g.scalar, g.tensor, g.sync
    RELU, COPY = ActivationFunctionType.Relu, ActivationFunctionType.Copy
    OP, FN = AluOpType, ActivationFunctionType

    def arrivals(form):
        return sum(len(es) for s in range(N) if s != rank for f, _p, trs in plan(topo, cores, s) if f == form
                   for d, _k, es in trs if d == rank)
    NQ, NS = arrivals("q"), arrivals("s")
    far, near, mate = order(topo, cores, rank)
    GROUPS = {"a": (0, len(far)), "b": (len(far), N - 1)}

    def slot_runs(t):
        at = BASE + (t - 1) * N * CAPP
        return [(at + a * CAPP, at + b * CAPP) for a, b in ((0, rank), (rank + 1, N)) if b > a]

    def batches(t):
        return [(a, b, min(a, b - LEAST)) for a, b in (CUTS if t < 3 else [(SENT, TILE)])]

    def table(q, out, src, groups, sem):
        for k in groups:
            q.dma_start(out(slice(16 * k, 16 * k + 16)), src[:, :]).then_inc(sem, 16)
    Y.dma_start(T.xt[:], T.x[:]).then_inc(S.ldx, 16)
    table(A, lambda p: T.sni[p], T.sn, range(0, 3), S.ldsn)
    table(Y, lambda p: T.sni[p], T.sn, range(3, 4), S.ldsn)
    table(Y, lambda p: T.kid[p, 0], T.lc, range(2), S.ldk)
    table(A, lambda p: T.kid[p, 1], T.rc, range(2), S.ldk)
    Y.dma_start(T.wlt[:, 0:1024], T.wl[:, 0:1024]).then_inc(S.ldwl, 16)
    A.dma_start(T.wlt[:, 1024:2048], T.wl[:, 1024:2048]).then_inc(S.ldwl, 16)
    Y.dma_start(T.wrt[:, 0:1024], T.wr[:, 0:1024]).then_inc(S.ldwr, 16)
    Y.dma_start(T.wrt[:, 1024:2048], T.wr[:, 1024:2048]).then_inc(S.ldwr2, 16)

    def carry(t, u, runs, sem):
        for a, b in runs:
            Y.dma_start(T["w%dq" % u][:, a:b].bitcast(dt.uint8), T["w%dq" % t][:, a:b].bitcast(dt.uint8)).then_inc(sem, 16)
            Y.dma_start(T["w%ds" % u][:, a:b], T["w%ds" % t][:, a:b]).then_inc(sem, 16)
        return 32 * len(runs)
    Y.wait_ge(S.qx2, 1)
    Y.wait_ge(S.arq1, NQ)
    Y.wait_ge(S.ars1, NS)
    C3 = carry(2, 3, slot_runs(1) + [(0, LEAVES)], S.c3)
    C4 = carry(2, 4, slot_runs(1) + [(0, LEAVES)], S.c4)
    Y.wait_ge(S.qn1_1, 1)
    Y.wait_ge(S.arq2, NQ)
    Y.wait_ge(S.ars2, NS)
    C4 += carry(3, 4, slot_runs(2) + [(first(1), first(2))], S.c4)
    Y.dma_start(T.vt[:], T.v[:]).then_inc(S.ldv, 16)

    HALVES = (slice(0, 64), slice(64, 128))
    QUARTERS = [slice(32 * a, 32 * a + 32) for a in range(4)]

    def slots_list(ds, k, sem):
        step = ds[-1] - ds[0] or 1
        for half in HALVES:
            V.tensor_copy(T.sl[half, :, 2 * k:2 * (k + len(ds))],
                          T.sni[0:64, :, ds[0]:ds[-1] + 1:step, :]).then_inc(sem, 1)

    def pick(q, out, at, n, t, wide, off, sem):
        if q is V:
            V.tensor_copy(T[out + "q"][:, at:at + n].bitcast(dt.uint32),
                          T["w%dq" % t][:, 0:wide].bitcast(dt.uint32).indirect(off)).then_inc(sem, 1)
        else:
            A.activation(T[out + "s"][:, at:at + n], T["w%ds" % t][:, 0:wide].indirect(off), COPY).then_inc(sem, 1)

    def pick_slots(q, t, name):
        a, b = GROUPS[name]
        off = T.sl[:, 0, 2 * a:2 * b] if t == 1 else T.sm[:, t - 2, 2 * a:2 * b]
        pick(q, "o%d" % t, a * CAPP, (b - a) * CAPP, t, WIDE[t], off, S["p%s%s%d" % (name, "q" if q is V else "s", t)])

    def pick_kids(q, t, b, side):
        a, z, _m = batches(t)[b]
        pick(q, "%s%d" % ("lr"[side], t), a, z - a, t + 1, WIDE[t + 1], T.lr[:, side, t - 1, a // 16:z // 16],
             S["p%s%d_%d" % ("lr"[side], t, b)])

    def banks(t, b):
        return T.psa if b == 0 else T.psb

    def evict(q, t, b, i):
        a, z, m = batches(t)[b]
        src, out = banks(t, b)[:, 512 * i + a - m:512 * i + z - m], T["h%d" % t][:, 4 * a + i:4 * z:4]
        q.wait_ge(S["m%d%d_%d" % (i, t, b)], 1)
        if q is V:
            V.tensor_scalar(out, src, 0.0, 0.05, OP.max, OP.mult).then_inc(S["ev%d_%d" % (t, b)], 1)
        else:
            A.activation(out, src, RELU, scale=0.05).then_inc(S["ev%d_%d" % (t, b)], 1)

    def quant(name, at, tile, a, z, sem):
        V.quantize_mx(T[name + "q"][:, at:at + z - a], T[name + "s"][:, at:at + z - a], tile[:, 4 * a:4 * z]).then_inc(sem, 1)

    V.memset(T.lr[0:32], 0).then_inc(S.k1, 1)
    V.memset(T.d0[:], 0.0).then_inc(S.k1, 1)
    V.memset(T.d1[:], 0.0).then_inc(S.k1, 1)
    for k, half in enumerate(HALVES):
        V.memset(T.n0[half, :], float(first(k + 1))).then_inc(S.k1, 1)
    V.wait_ge(S.iot, 3)
    V.tensor_scalar(T.b4[:], T.pi[:, 0:KIDS], 4, 1, OP.logical_shift_right, OP.bitwise_and).then_inc(S.k1, 1)
    V.tensor_scalar(T.pa[:], T.pi[:, 0:1], 14, None, OP.bitwise_and).then_inc(S.k1, 1)
    V.tensor_scalar(T.pm[:], T.pi[:], 15, None, OP.bitwise_and).then_inc(S.k1, 1)
    V.wait_ge(S.k1, 8)
    V.tensor_tensor(T.cbi[:], T.ev[:], T.b4[:], OP.add).then_inc(S.k2, 1)
    V.tensor_tensor(T.s1[:], T.pa[:], T.b4[:, 0:1], OP.add).then_inc(S.k2, 1)
    V.tensor_tensor(T.jf[:], T.jj[:], T.pm[:], OP.add).then_inc(S.k2, 1)
    V.wait_ge(S.k2, 3)
    V.tensor_copy(T.cb[:], T.cbi[:]).then_inc(S.k3, 1)
    for k, half in enumerate(HALVES):
        V.tensor_scalar(T.co[half, 0:1], T.s1[half, :], 2, 2 * OFFS * k + 1, OP.mult, OP.add).then_inc(S.k3, 1)

    V.wait_ge(S.ldsn, 64)
    slots_list(far, GROUPS["a"][0], S.so1)
    V.wait_ge(S.ldx, 16)
    quant("w1", 0, T.xt, 0, LEAVES, S.qx1)
    V.wait_ge(S.so1, 2)
    V.wait_ge(S.qx1, 1)
    pick_slots(V, 1, "a")
    V.wait_ge(S.ldk, 64)
    for a, part in enumerate(QUARTERS):
        V.tensor_copy(T.pkw[part, :], T.kid[0:32, a % 2, KIDS * (a // 2):KIDS * (a // 2 + 1)]).then_inc(S.win, 1)
    slots_list(near, len(far), S.so2)
    slots_list(mate, len(far + near), S.so2)
    V.wait_ge(S.so2, 4)
    pick_slots(V, 1, "b")

    ODD, EVEN = slice(1, 4 * OFFS, 2), slice(0, 4 * OFFS, 2)
    V.wait_ge(S.k3, 3)
    V.tensor_copy(T.d1[:, ODD], T.sl[:, 1:3, :]).then_inc(S.m1, 1)
    V.wait_ge(S.ab, 1)
    V.transpose(T.ff[:], T.bb[:]).then_inc(S.t1, 1)
    V.wait_ge(S.m1, 1)
    V.tensor_scalar(T.off[:], T.d1[:].indirect(T.co[:, 0:1]), T.n0[:], float(NODES - 1), OP.subtract, OP.min).then_inc(S.dof, 1)
    V.tensor_copy(T.lr[0:32, :, :, OFFS:], T.kid[0:32]).then_inc(S.d5, 1)
    quant("w2", 0, T.xt, 0, LEAVES, S.qx2)
    V.wait_ge(S.dof, 1)
    V.tensor_tensor(T.d1[:, EVEN], T.jf[:], T.d1[:, ODD], OP.subtract).then_inc(S.m2, 1)
    V.wait_ge(S.ldwl, 32)
    quant("wl", 0, T.wlt, 0, 512, S.qwl)
    V.wait_ge(S.ag, 1)
    V.transpose(T.gt[:], T.gg[:]).then_inc(S.t2, 1)
    V.wait_ge(S.m2, 1)
    V.wait_ge(S.new, 1)
    V.tensor_tensor_scan(T.sc[:], T.d0[:], T.d1[:, 0:4 * OFFS], 0.0, OP.mult, OP.add).then_inc(S.m3, 1)
    V.wait_ge(S.t2, 1)
    for a, part in enumerate(QUARTERS):
        V.tensor_copy(T.lr[0:32, a % 2, a // 2, 0:OFFS], T.gt[part, 0:SENT:16]).then_inc(S.d5, 1)
    V.wait_ge(S.d5, 5)
    V.tensor_copy(T.lr[32:64], T.lr[0:32]).then_inc(S.d6, 1)
    V.wait_ge(S.m3, 1)
    V.tensor_copy(T.sm[:], T.sc[:, ODD]).then_inc(S.dsm, 1)
    V.wait_ge(S.ldwr, 16)
    quant("wr", 0, T.wrt, 0, 256, S.qwr)
    V.wait_ge(S.d6, 1)
    V.tensor_copy(T.lr[64:128], T.lr[0:64]).then_inc(S.d7, 1)

    def ready(q, t):
        if t == 1:
            q.wait_ge(S.qx2, 1)
            q.wait_ge(S.d7, 1)
            q.wait_ge(S.dsm, 1)
        if t == 2:
            q.wait_ge(S.qn1_1, 1)
            q.wait_ge(S.c3, C3)
        if t == 3:
            q.wait_ge(S.qn2_1, 1)
            q.wait_ge(S.c4, C4)

    for t in (1, 2):
        h, w = T["h%d" % t], "w%d" % (t + 1)
        ready(V, t)
        V.wait_ge(S["arq%d" % t], NQ)
        pick_kids(V, t, 0, 0)
        pick_kids(V, t, 0, 1)
        if t == 1:
            V.wait_ge(S.ldwr2, 16)
            quant("wr", 256, T.wrt, 256, 512, S.qwr2)
        pick_kids(V, t, 1, 0)
        for i in (1, 3):
            evict(V, t, 0, i)
        V.wait_ge(S["pl%d_1" % t], 2)
        V.wait_ge(S["ev%d_0" % t], 4)
        quant(w, first(t), h, 0, SENT, S["qn%d_0" % t])
        V.wait_ge(S["qn%d_0" % t], 1)
        pick_slots(V, t + 1, "a")
        pick_slots(V, t + 1, "b")
        pick_kids(V, t, 1, 1)
        for i in (1, 3):
            evict(V, t, 1, i)
        V.wait_ge(S["ev%d_1" % t], 4)
        quant("w%d" % (t + 2), first(t), h, SENT, TILE, S["qn%d_1" % t])
    ready(V, 3)
    V.wait_ge(S.arq3, NQ)
    pick_kids(V, 3, 0, 0)
    pick_kids(V, 3, 0, 1)
    V.wait_ge(S.ldv, 16)
    quant("v", 0, T.vt, 0, 128, S.qv)
    for i in (1, 3):
        evict(V, 3, 0, i)
    V.wait_ge(S.ev3_0, 4)
    quant("h", 0, T.h3, SENT, TILE, S.qh)
    V.wait_ge(S.mmy, 1)
    V.tensor_copy(T.ys[:], T.psb[:, 0:NODES]).then_inc(S.evy, 1)

    A.wait_ge(S.so1, 2)
    A.wait_ge(S.qx1, 1)
    pick_slots(A, 1, "a")
    A.wait_ge(S.win, 4)
    A.wait_ge(S.k3, 3)
    A.activation(T.bb[:], T.pkw[:].indirect(T.cb[:]), COPY).then_inc(S.ab, 1)
    A.wait_ge(S.so2, 4)
    pick_slots(A, 1, "b")
    A.wait_ge(S.m1, 1)
    for t in (1, 2):
        A.activation(T.r1[:, OFFS * (t - 1):OFFS * t], T.d1[:, 2 * OFFS * (t - 1) + 1:2 * OFFS * t:2], FN.Abs,
                     bias=-(first(t) + (NODES - 1) / 2)).then_inc(S.a1, 1)
    A.wait_ge(S.t1, 1)
    A.wait_ge(S.dof, 1)
    A.activation(T.gg[:], T.ff[:].indirect(T.off[:, 0:OFFS]), COPY).then_inc(S.ag, 1)
    A.wait_ge(S.a1, 2)
    A.activation(T.r2[:], T.r1[:], FN.Sign, bias=NODES / 2, scale=-1.0).then_inc(S.a2, 1)
    A.wait_ge(S.a2, 1)
    A.activation(T.d0[:, ODD], T.r2[:], RELU).then_inc(S.new, 1)
    for t in (1, 2):
        ready(A, t)
        A.wait_ge(S["ars%d" % t], NS)
        pick_kids(A, t, 0, 0)
        pick_kids(A, t, 0, 1)
        pick_kids(A, t, 1, 0)
        for i in (0, 2):
            evict(A, t, 0, i)
        A.wait_ge(S["qn%d_0" % t], 1)
        pick_slots(A, t + 1, "a")
        pick_slots(A, t + 1, "b")
        pick_kids(A, t, 1, 1)
        for i in (0, 2):
            evict(A, t, 1, i)
    ready(A, 3)
    A.wait_ge(S.ars3, NS)
    pick_kids(A, 3, 0, 0)
    pick_kids(A, 3, 0, 1)
    for i in (0, 2):
        evict(A, 3, 0, i)

    E.wait_ge(S.qwl, 1)
    for t in (1, 2, 3):
        for b, (_a, z, m) in enumerate(batches(t)):
            for side, w in enumerate(("wl", "wr")):
                if (t, b, side) == (1, 0, 1):
                    E.wait_ge(S.qwr, 1)
                name = "%s%d" % ("lr"[side], t)
                E.wait_ge(S["p%s_%d" % (name, b)], 2)
                for i in range(4):
                    if (t, b, side, i) == (1, 0, 1, 2):
                        E.wait_ge(S.qwr2, 1)
                    mm = E.matmul_mx(banks(t, b)[:, 512 * i:512 * i + z - m], T[w + "q"][:, 128 * i:128 * i + 128],
                                     T[w + "s"][:, 128 * i:128 * i + 128], T[name + "q"][:, m:z], T[name + "s"][:, m:z],
                                     side == 0, side == 1)
                    if side:
                        mm.then_inc(S["m%d%d_%d" % (i, t, b)], 1)
    E.wait_ge(S.qv, 1)
    E.wait_ge(S.qh, 1)
    E.matmul_mx(T.psb[:, 0:NODES], T.vq[:], T.vs[:], T.hq[:], T.hs[:], True, True).then_inc(S.mmy, 1)

    g.iota(T.pi[:], [[0, 2 * OFFS]], 0, 1).then_inc(S.iot, 1)
    g.iota(T.ev[:], [[2, KIDS // 2], [0, 2]], 0, 0).then_inc(S.iot, 1)
    g.iota(T.jj[:], [[NODES, 2], [16, OFFS]], LEAVES, 0).then_inc(S.iot, 1)
    left = 0
    for t in (1, 2, 3):
        for form, picked, sends in plan(topo, cores, rank):
            trs = []
            for d, k, es in sends:
                rid, pid, _se = topo.addr(cores[d])
                at = BASE + ((t - 1) * N + rank) * CAPP
                src = T["o%d%s" % (t, form)][:, CAPP * k:CAPP * k + CAPP]
                dst = T["w%d%s" % (t + 1, form)][:, at:at + CAPP]
                if form == "q":
                    src, dst = src.bitcast(dt.uint8), dst.bitcast(dt.uint8)
                left += len(es)
                trs.append(RemoteDMATransfer(dst_ids=[DstId(rid=rid, pnc=pid)], dma_engine_mask=bits(es),
                                             remote_sem=S["ar%s%d" % (form, t)], src=src, dst=dst))
            g.wait_ge(S["%s%s%d" % (picked, form, t)], 1)
            g.remote_dma_fused(trs, local_sem=S.left)
    g.wait_ge(S.left, left)

    Y.wait_ge(S.evy, 1)
    Y.dma_start(T.y[:], T.ys[:]).then_inc(S.sty, 16)
    Y.wait_ge(S.sty, 16)
